import numpy as np
import ml_dtypes


def mxq(x, axis, fmt="e4m3"):
    dtype, down = {"e4m3": (ml_dtypes.float8_e4m3fn, 7), "e5m2": (ml_dtypes.float8_e5m2, 14)}[fmt]
    v = np.moveaxis(np.asarray(x, np.float32).astype(ml_dtypes.bfloat16).astype(np.float64), axis, -1)
    blocks = v.reshape(v.shape[:-1] + (-1, 32))
    amax = np.abs(blocks).max(-1, keepdims=True)
    byte = np.maximum(np.where(amax > 0, np.frexp(amax)[1] - 1 + 127, 0) - down, 1)
    scale = np.exp2(byte - 127.0)
    codes = (blocks / scale).astype(np.float32).astype(dtype).astype(np.float64)
    return np.moveaxis((codes * scale).reshape(v.shape), -1, axis)


WIDE = False


def mx_kscale(k):
    if not WIDE:
        return np.ones(k)
    levels = np.array([18, -18])
    if k % 512:
        return np.exp2(np.random.permutation(np.resize(levels, k // 32))).repeat(32)
    a = np.empty((k // 512, 16))
    for p in range(k // 512):
        a[p, :8] = np.random.permutation(np.resize(levels, 8))
        for g in range(8):
            far = levels[np.abs(levels - a[p, g]) >= 10]
            a[p, g + 8] = far[np.random.randint(len(far))]
    return np.exp2(a.ravel()).repeat(32)


def f64(x):
    return np.asarray(x).astype(np.float64)


def striped(idx):
    return np.tile(np.asarray(idx).reshape(-1, 16).T, (8, 1)).astype(np.uint16)


def unstriped(offs):
    return offs[:16].T.reshape(-1).astype(np.int64)

def planes(y):
    n, m = y.shape
    v = y.astype(np.float32).astype(ml_dtypes.bfloat16).astype(np.float64).reshape(n // 32, 32, m)
    top = np.abs(v).max(1)
    byte = np.clip(np.where(top > 0, np.frexp(top)[1] - 1 + 127 - 7, 1), 1, 254)
    codes = (v * np.exp2(127.0 - byte)[:, None, :]).reshape(n, m).astype(np.float32).astype(ml_dtypes.float8_e4m3fn).view(np.uint8)
    words = codes.reshape(n // 512, 128, 4, m).transpose(0, 1, 3, 2)
    return np.ascontiguousarray(words), np.ascontiguousarray(byte.astype(np.uint8).reshape(n // 512, 16, m))


B, N, T, D, R = 1, 512, 2048, 512, 512


def setup_inputs():
    n = np.random.standard_normal
    idx = np.random.permutation(T)[:B * N]
    s = mx_kscale(D)[:, None]
    u = np.ones(T)
    u[idx] = mx_kscale(B * N)
    r = np.random.uniform(0.5, 2.0, T) * u
    x = n((B, D, R))
    return {
        "xT": (x * s).astype(np.float32),
        "wT": (n((D, T)) * (1.00 / np.sqrt(D)) / s / r).astype(np.float32),
        "y": n((B, R, N)).astype(np.float32),
        "wt": (np.random.uniform(0.5, 1.5, (B, R, 1)) * 1.0 / np.sqrt(R)).astype(np.float32),
        "ts": np.tile(r, (128, 1)).astype(np.float32),
        "offs": striped(idx),
    }


def reference(xT, wT, y, wt, ts, offs):
    idx = unstriped(offs)
    pick = lambda x: x[:, idx].reshape(x.shape[0], B, N).transpose(1, 0, 2)
    w = pick(f64(wT))
    a = mxq(f64(xT), 1, "e4m3").transpose(0, 2, 1) @ mxq(w, 1, "e4m3")
    ts_ = pick(f64(ts))[:, :1, :]
    a = a * ts_
    g = f64(wt) * (a - f64(y))
    g = g * ts_
    gx = mxq(g, 2, "e5m2") @ mxq(w, 2, "e4m3").transpose(0, 2, 1)
    out_0 = gx
    return (out_0,) + planes(out_0[0])

@@ -1,0 +1,179 @@
+from contextlib import ExitStack
+
+import concourse.mybir as mybir
+from concourse.masks import make_identity
+
+N, T, D, R = 512, 2048, 512, 512
+P = 128
+PACK = 4
+
+F32 = mybir.dt.float32
+BF16 = mybir.dt.bfloat16
+I32 = mybir.dt.int32
+U32 = mybir.dt.uint32
+U16 = mybir.dt.uint16
+U8 = mybir.dt.uint8
+E4M3 = mybir.dt.float8_e4m3fn_x4
+E5M2 = mybir.dt.float8_e5m2_x4
+MULT = mybir.AluOpType.mult
+COPY = mybir.ActivationFunctionType.Copy
+
+FLOPS = 2 * 2 * R * N * D
+BYTES = 4 * (D * R + D * T + R * N + R + T + R * D) + 2 * P * (N // 16) + R * D + (R // 32) * D
+
+VECTOR_COLS = 20
+
+
+def tile_attend_gsq_pl_x_ts_kernel(tc, xT, wT, y, wt, ts, offs, out_0, out_1, out_2):
+    nc = tc.nc
+    with ExitStack() as ctx:
+        sb = ctx.enter_context(tc.tile_pool(name="sb", bufs=1))
+        acc = ctx.enter_context(tc.psum_pool(name="acc", bufs=4))
+        turn = ctx.enter_context(tc.psum_pool(name="turn", bufs=4))
+
+        offsets = sb.tile([P, N // 16], U16, name="offsets")
+        nc.sync.dma_start(offsets[:], offs)
+
+        w_planes = wT.rearrange("(p j) c -> p j c", j=PACK)
+        w_raw = [sb.tile([P, T], F32, name="w_raw%d" % j) for j in range(PACK)]
+        nc.sync.dma_start(out=w_raw[0][:], in_=w_planes[:, 0, :])
+
+        ts_row = sb.tile([P, T], F32, name="ts_row")
+        nc.vector.memset(ts_row[:, : T // 2], 0.0)
+        nc.gpsimd.memset(ts_row[:, T // 2 :], 0.0)
+        nc.sync.dma_start(out=ts_row[0:1, :], in_=ts[0:1, :])
+        wt_cols = sb.tile([P, PACK], F32, name="wt_cols")
+        nc.sync.dma_start(out=wt_cols[:], in_=wt[0].rearrange("(q t) o -> q (t o)", t=PACK))
+
+        for j in range(1, PACK):
+            nc.sync.dma_start(out=w_raw[j][:], in_=w_planes[:, j, :])
+        x_planes = xT[0].rearrange("(p j) r -> p j r", j=PACK)
+        x_raw = [sb.tile([P, 2, R], F32, name="x_raw%d" % k) for k in range(2)]
+        for k in range(2):
+            nc.sync.dma_start(out=x_raw[k][:], in_=x_planes[:, 2 * k : 2 * k + 2, :])
+        y_rows = y[0].rearrange("(q t) i -> q t i", t=PACK)
+        y_raw = [sb.tile([P, N], F32, name="y_raw%d" % t) for t in range(PACK)]
+        for t in range(PACK):
+            nc.sync.dma_start(out=y_raw[t][:], in_=y_rows[:, t, :])
+
+        ident = sb.tile([P, P], F32, name="ident")
+        make_identity(nc, ident[:])
+        neg_wt = sb.tile([P, PACK], F32, name="neg_wt")
+        nc.vector.tensor_scalar(neg_wt[:], wt_cols[:], -1.0, None, MULT)
+
+        ts_picked = sb.tile([P, N], F32, name="ts_picked")
+        nc.vector.tensor_copy(ts_picked[:], ts_row[:].indirect(offsets[:]))
+        bank = turn.tile([P, PACK, P], F32, name="turn_bank")
+        for u in range(PACK):
+            nc.tensor.transpose(bank[:, u, :], ts_picked[:, u:N:PACK], ident[:])
+        ts_cols = sb.tile([P, 1, PACK], F32, name="ts_cols")
+        nc.vector.tensor_copy(ts_cols[:, 0, :], bank[:, :, 0])
+        bank = turn.tile([P, PACK, P], F32, name="turn_bank")
+        for u in range(PACK):
+            nc.tensor.transpose(bank[:, u, :], ts_cols[:, 0, u : u + 1].to_broadcast([P, P]), ident[:])
+        ts_rows = sb.tile([P, N], F32, name="ts_rows")
+        nc.scalar.copy(ts_rows[:], bank[:].rearrange("p u s -> p (u s)"))
+
+        picked = [sb.tile([P, 2, N], BF16, name="picked%d" % k, align_bytes=64) for k in range(2)]
+        w_by_d = sb.tile([P, N * PACK], BF16, name="w_by_d", align_bytes=64)
+        w_by_slot = sb.tile([P, D * PACK], BF16, name="w_by_slot", align_bytes=64)
+        for k in range(2):
+            for e in range(2):
+                j = 2 * k + e
+                if j < PACK - 1:
+                    nc.vector.tensor_copy(picked[k][:, e, :], w_raw[j][:].indirect(offsets[:]))
+                else:
+                    cut = 16 * VECTOR_COLS
+                    nc.vector.tensor_copy(picked[k][:, e, :cut], w_raw[j][:].indirect(offsets[:, :VECTOR_COLS]))
+                    nc.scalar.activation(picked[k][:, e, cut:], w_raw[j][:].indirect(offsets[:, VECTOR_COLS:]), COPY)
+            nc.vector.tensor_copy(
+                w_by_d[:].rearrange("p (u s j) -> p s j u", u=PACK, j=PACK)[:, :, 2 * k : 2 * k + 2, :],
+                picked[k][:].rearrange("p e (s u) -> p s e u", u=PACK),
+            )
+            bank = turn.tile([P, PACK, P], F32, name="turn_bank")
+            for e in range(2):
+                words = picked[k][:, e, :].bitcast(F32)
+                for v in range(2):
+                    nc.tensor.transpose(bank[:, 2 * e + v, :], words[:, v : N // 2 : 2], ident[:])
+            nc.scalar.copy(
+                w_by_slot[:].bitcast(F32).rearrange("s (p j v) -> s p j v", j=PACK, v=2)[:, :, 2 * k : 2 * k + 2, :],
+                bank[:].rearrange("s (e v) p -> s p e v", v=2),
+            )
+        wd_codes = sb.tile([P, N], U32, name="wd_codes", align_bytes=64)
+        wd_scales = sb.tile([P, N], U8, name="wd_scales", align_bytes=64)
+        nc.vector.quantize_mx(out=wd_codes[:].bitcast(E4M3), scales=wd_scales[:], in_=w_by_d[:])
+
+        x_by_d = sb.tile([P, R * PACK], BF16, name="x_by_d", align_bytes=64)
+        x_view = x_by_d[:].rearrange("p (t q j) -> p q j t", t=PACK, j=PACK)
+        nc.scalar.copy(x_view[:, :, 0:2, :], x_raw[0][:].rearrange("p e (q t) -> p q e t", t=PACK))
+        nc.vector.tensor_copy(x_view[:, :, 2:4, :], x_raw[1][:].rearrange("p e (q t) -> p q e t", t=PACK))
+        scores = []
+        for t in range(PACK):
+            x_codes = sb.tile([P, P], U32, name="x_codes%d" % t, align_bytes=64)
+            x_scales = sb.tile([P, P], U8, name="x_scales%d" % t, align_bytes=64)
+            nc.vector.quantize_mx(out=x_codes[:].bitcast(E4M3), scales=x_scales[:], in_=x_by_d[:, t * P * PACK : (t + 1) * P * PACK])
+            a = acc.tile([P, N], F32, name="acc_bank")
+            nc.tensor.matmul_mx(out=a[:], lhsT=x_codes[:].bitcast(E4M3), lhsT_scale=x_scales[:],
+                                rhs=wd_codes[:].bitcast(E4M3), rhs_scale=wd_scales[:], start=True, stop=True)
+            scores.append(a)
+
+        ws_codes = sb.tile([P, D], U32, name="ws_codes", align_bytes=64)
+        ws_scales = sb.tile([P, D], U8, name="ws_scales", align_bytes=64)
+        nc.vector.quantize_mx(out=ws_codes[:].bitcast(E4M3), scales=ws_scales[:], in_=w_by_slot[:])
+
+        terms = []
+        for t in range(PACK):
+            target = sb.tile([P, N], F32, name="target%d" % t)
+            nc.scalar.activation(target[:].rearrange("q (u s) -> q s u", u=PACK),
+                                 y_raw[t][:].rearrange("q (s u) -> q s u", u=PACK), COPY, scale=neg_wt[:, t : t + 1])
+            fitted = sb.tile([P, N], F32, name="fitted%d" % t)
+            nc.vector.scalar_tensor_tensor(fitted[:], scores[t][:], wt_cols[:, t : t + 1], ts_rows[:], MULT, MULT)
+            terms.append((target, fitted))
+
+        g_banks = []
+        for t in range(PACK):
+            bank = turn.tile([P, PACK, P], F32, name="turn_bank")
+            for n, term in enumerate(terms[t]):
+                for u in range(PACK):
+                    nc.tensor.matmul(bank[:, u, :], lhsT=term[:, u * P : (u + 1) * P], rhs=ident[:], is_transpose=True,
+                                     start=(n == 0 and u == 0), stop=(n == 1 and u == PACK - 1))
+            g_banks.append(bank)
+
+        out_rows = out_0[0].rearrange("(q t) d -> q t d", t=PACK)
+        result = [sb.tile([P, 2, D], F32, name="result%d" % k) for k in range(2)]
+        o_by_row = sb.tile([P, D * PACK], BF16, name="o_by_row", align_bytes=64)
+        h_tiles = []
+
+        def weigh(t):
+            h = sb.tile([P, P * PACK], BF16, name="h%d" % t, align_bytes=64)
+            nc.vector.tensor_tensor(h[:].rearrange("s (q u) -> s q u", u=PACK), g_banks[t][:].rearrange("s u q -> s q u"),
+                                    ts_cols[:].to_broadcast([P, P, PACK]), MULT)
+            h_tiles.append(h)
+
+        def multiply(t):
+            h_codes = sb.tile([P, P], U32, name="h_codes%d" % t, align_bytes=64)
+            h_scales = sb.tile([P, P], U8, name="h_scales%d" % t, align_bytes=64)
+            nc.vector.quantize_mx(out=h_codes[:].bitcast(E5M2), scales=h_scales[:], in_=h_tiles[t][:])
+            gx = acc.tile([P, D], F32, name="acc_bank")
+            nc.tensor.matmul_mx(out=gx[:], lhsT=h_codes[:].bitcast(E5M2), lhsT_scale=h_scales[:],
+                                rhs=ws_codes[:].bitcast(E4M3), rhs_scale=ws_scales[:], start=True, stop=True)
+            nc.scalar.copy(result[t // 2][:, t % 2, :], gx[:])
+            nc.sync.dma_start(out=out_rows[:, t, :], in_=result[t // 2][:, t % 2, :])
+
+        weigh(0)
+        for t in range(1, PACK):
+            weigh(t)
+            multiply(t - 1)
+        multiply(PACK - 1)
+
+        o_view = o_by_row[:].rearrange("q (d t) -> q d t", t=PACK)
+        for k in range(2):
+            nc.vector.tensor_copy(o_view[:, :, 2 * k : 2 * k + 2], result[k][:].rearrange("q e d -> q d e"))
+        o_codes = sb.tile([P, D], U32, name="o_codes", align_bytes=64)
+        o_scales = sb.tile([P, D], U8, name="o_scales", align_bytes=64)
+        nc.vector.quantize_mx(out=o_codes[:].bitcast(E4M3), scales=o_scales[:], in_=o_by_row[:])
+        nc.sync.dma_start(out=out_1[0].rearrange("p d l -> p (d l)").bitcast(I32), in_=o_codes[:].bitcast(I32))
+        for quad in range(4):
+            queue = nc.scalar if quad % 2 == 0 else nc.sync
+            queue.dma_start(out=out_2[0, 4 * quad : 4 * quad + 4, :].bitcast(I32),
+                            in_=o_scales[32 * quad : 32 * quad + 4, :].bitcast(I32))

@@ -16,12 +16,14 @@ U8 = mybir.dt.uint8
 E4M3 = mybir.dt.float8_e4m3fn_x4
 E5M2 = mybir.dt.float8_e5m2_x4
 MULT = mybir.AluOpType.mult
+ADD = mybir.AluOpType.add
 COPY = mybir.ActivationFunctionType.Copy
 
 FLOPS = 2 * 2 * R * N * D
 BYTES = 4 * (D * R + D * T + R * N + R + T + R * D) + 2 * P * (N // 16) + R * D + (R // 32) * D
 
-VECTOR_COLS = 20
+PE_SUMS = 2
+VECTOR_COLS = 16
 
 
 def tile_attend_gsq_pl_x_ts_kernel(tc, xT, wT, y, wt, ts, offs, out_0, out_1, out_2):
@@ -31,26 +33,25 @@ def tile_attend_gsq_pl_x_ts_kernel(tc, xT, wT, y, wt, ts, offs, out_0, out_1, ou
         acc = ctx.enter_context(tc.psum_pool(name="acc", bufs=4))
         turn = ctx.enter_context(tc.psum_pool(name="turn", bufs=4))
 
+        w_planes = wT.rearrange("(p j) c -> p j c", j=PACK)
+        w_raw = [sb.tile([P, T], F32, name="w_raw%d" % j, tag="w_raw%d" % j, align_bytes=64) for j in range(PACK)]
+        nc.sync.dma_start(out=w_raw[0][:], in_=w_planes[:, 0, :])
         offsets = sb.tile([P, N // 16], U16, name="offsets")
         nc.sync.dma_start(offsets[:], offs)
 
-        w_planes = wT.rearrange("(p j) c -> p j c", j=PACK)
-        w_raw = [sb.tile([P, T], F32, name="w_raw%d" % j) for j in range(PACK)]
-        nc.sync.dma_start(out=w_raw[0][:], in_=w_planes[:, 0, :])
-
+        wt_cols = sb.tile([P, PACK], F32, name="wt_cols")
+        nc.scalar.dma_start(out=wt_cols[:], in_=wt[0].rearrange("(q t) o -> q (t o)", t=PACK))
         ts_row = sb.tile([P, T], F32, name="ts_row")
         nc.vector.memset(ts_row[:, : T // 2], 0.0)
         nc.gpsimd.memset(ts_row[:, T // 2 :], 0.0)
         nc.sync.dma_start(out=ts_row[0:1, :], in_=ts[0:1, :])
-        wt_cols = sb.tile([P, PACK], F32, name="wt_cols")
-        nc.sync.dma_start(out=wt_cols[:], in_=wt[0].rearrange("(q t) o -> q (t o)", t=PACK))
 
         for j in range(1, PACK):
             nc.sync.dma_start(out=w_raw[j][:], in_=w_planes[:, j, :])
         x_planes = xT[0].rearrange("(p j) r -> p j r", j=PACK)
-        x_raw = [sb.tile([P, 2, R], F32, name="x_raw%d" % k) for k in range(2)]
-        for k in range(2):
-            nc.sync.dma_start(out=x_raw[k][:], in_=x_planes[:, 2 * k : 2 * k + 2, :])
+        x_raw = [sb.tile([P, PACK, R // 2], F32, name="x_raw%d" % h) for h in range(2)]
+        for h in range(2):
+            nc.sync.dma_start(out=x_raw[h][:], in_=x_planes[:, :, h * (R // 2) : (h + 1) * (R // 2)])
         y_rows = y[0].rearrange("(q t) i -> q t i", t=PACK)
         y_raw = [sb.tile([P, N], F32, name="y_raw%d" % t) for t in range(PACK)]
         for t in range(PACK):
@@ -59,67 +60,78 @@ def tile_attend_gsq_pl_x_ts_kernel(tc, xT, wT, y, wt, ts, offs, out_0, out_1, ou
         ident = sb.tile([P, P], F32, name="ident")
         make_identity(nc, ident[:])
         neg_wt = sb.tile([P, PACK], F32, name="neg_wt")
-        nc.vector.tensor_scalar(neg_wt[:], wt_cols[:], -1.0, None, MULT)
+        nc.scalar.activation(neg_wt[:], wt_cols[:], COPY, scale=-1.0)
 
         ts_picked = sb.tile([P, N], F32, name="ts_picked")
-        nc.vector.tensor_copy(ts_picked[:], ts_row[:].indirect(offsets[:]))
+        nc.scalar.activation(ts_picked[:], ts_row[:].indirect(offsets[:]), COPY)
         bank = turn.tile([P, PACK, P], F32, name="turn_bank")
         for u in range(PACK):
             nc.tensor.transpose(bank[:, u, :], ts_picked[:, u:N:PACK], ident[:])
         ts_cols = sb.tile([P, 1, PACK], F32, name="ts_cols")
-        nc.vector.tensor_copy(ts_cols[:, 0, :], bank[:, :, 0])
+        nc.scalar.copy(ts_cols[:, 0, :], bank[:, :, 0])
         bank = turn.tile([P, PACK, P], F32, name="turn_bank")
         for u in range(PACK):
             nc.tensor.transpose(bank[:, u, :], ts_cols[:, 0, u : u + 1].to_broadcast([P, P]), ident[:])
         ts_rows = sb.tile([P, N], F32, name="ts_rows")
         nc.scalar.copy(ts_rows[:], bank[:].rearrange("p u s -> p (u s)"))
 
-        picked = [sb.tile([P, 2, N], BF16, name="picked%d" % k, align_bytes=64) for k in range(2)]
+        picked = [sb.tile([P, 2 * N], BF16, name="picked%d" % k, align_bytes=64) for k in range(2)]
         w_by_d = sb.tile([P, N * PACK], BF16, name="w_by_d", align_bytes=64)
-        w_by_slot = sb.tile([P, D * PACK], BF16, name="w_by_slot", align_bytes=64)
-        for k in range(2):
-            for e in range(2):
-                j = 2 * k + e
-                if j < PACK - 1:
-                    nc.vector.tensor_copy(picked[k][:, e, :], w_raw[j][:].indirect(offsets[:]))
-                else:
-                    cut = 16 * VECTOR_COLS
-                    nc.vector.tensor_copy(picked[k][:, e, :cut], w_raw[j][:].indirect(offsets[:, :VECTOR_COLS]))
-                    nc.scalar.activation(picked[k][:, e, cut:], w_raw[j][:].indirect(offsets[:, VECTOR_COLS:]), COPY)
-            nc.vector.tensor_copy(
-                w_by_d[:].rearrange("p (u s j) -> p s j u", u=PACK, j=PACK)[:, :, 2 * k : 2 * k + 2, :],
-                picked[k][:].rearrange("p e (s u) -> p s e u", u=PACK),
-            )
-            bank = turn.tile([P, PACK, P], F32, name="turn_bank")
-            for e in range(2):
-                words = picked[k][:, e, :].bitcast(F32)
-                for v in range(2):
-                    nc.tensor.transpose(bank[:, 2 * e + v, :], words[:, v : N // 2 : 2], ident[:])
-            nc.scalar.copy(
-                w_by_slot[:].bitcast(F32).rearrange("s (p j v) -> s p j v", j=PACK, v=2)[:, :, 2 * k : 2 * k + 2, :],
-                bank[:].rearrange("s (e v) p -> s p e v", v=2),
-            )
+        by_slot = [sb.tile([P, 2 * P * PACK], BF16, name="w_by_slot%d" % k, align_bytes=64) for k in range(2)]
+        ws_codes = sb.tile([P, D], U32, name="ws_codes", tag="w_raw2", align_bytes=64)
+        ws_scales = sb.tile([P, D], U8, name="ws_scales", align_bytes=64)
+        for j in range(PACK):
+            k, e = divmod(j, 2)
+            plane = picked[k][:, e * N : (e + 1) * N]
+            if j < PACK - 1:
+                nc.vector.tensor_copy(plane, w_raw[j][:].indirect(offsets[:]))
+            else:
+                cut = 16 * VECTOR_COLS
+                nc.vector.tensor_copy(plane[:, :cut], w_raw[j][:].indirect(offsets[:, :VECTOR_COLS]))
+                nc.scalar.activation(plane[:, cut:], w_raw[j][:].indirect(offsets[:, VECTOR_COLS:]), COPY)
+            if e == 1:
+                nc.vector.tensor_copy(
+                    w_by_d[:].rearrange("p (u s j) -> p s j u", u=PACK, j=PACK)[:, :, 2 * k : 2 * k + 2, :],
+                    picked[k][:].rearrange("p (e s u) -> p s e u", e=2, u=PACK),
+                )
+            bank = turn.tile([P, 2, P], F32, name="turn_bank")
+            for v in range(2):
+                nc.tensor.transpose(bank[:, v, :], plane.bitcast(F32)[:, v : N // 2 : 2], ident[:])
+            copy = nc.vector.tensor_copy if j == PACK - 1 else nc.scalar.copy
+            copy(by_slot[k][:].bitcast(F32).rearrange("s (c e p v) -> s e c p v", c=2, e=2, v=2)[:, e],
+                           bank[:].rearrange("s v (c p) -> s c p v", c=2))
+
+        def quantise_by_slot(k):
+            for c in range(2):
+                cols = slice(c * (D // 2) + k * P, c * (D // 2) + (k + 1) * P)
+                nc.vector.quantize_mx(out=ws_codes[:, cols].bitcast(E4M3), scales=ws_scales[:, cols],
+                                      in_=by_slot[k][:, c * P * PACK : (c + 1) * P * PACK])
+
+        quantise_by_slot(0)
         wd_codes = sb.tile([P, N], U32, name="wd_codes", align_bytes=64)
         wd_scales = sb.tile([P, N], U8, name="wd_scales", align_bytes=64)
         nc.vector.quantize_mx(out=wd_codes[:].bitcast(E4M3), scales=wd_scales[:], in_=w_by_d[:])
 
-        x_by_d = sb.tile([P, R * PACK], BF16, name="x_by_d", align_bytes=64)
-        x_view = x_by_d[:].rearrange("p (t q j) -> p q j t", t=PACK, j=PACK)
-        nc.scalar.copy(x_view[:, :, 0:2, :], x_raw[0][:].rearrange("p e (q t) -> p q e t", t=PACK))
-        nc.vector.tensor_copy(x_view[:, :, 2:4, :], x_raw[1][:].rearrange("p e (q t) -> p q e t", t=PACK))
+        x_by_d = [sb.tile([P, 2, P * PACK], BF16, name="x_by_d%d" % k, align_bytes=64) for k in range(2)]
+        for h in range(2):
+            for k in range(2):
+                nc.scalar.copy(x_by_d[k][:].rearrange("p e (q j) -> p q j e", j=PACK)[:, h * (P // 2) : (h + 1) * (P // 2), :, :],
+                     x_raw[h][:].rearrange("p j (q t) -> p q j t", t=PACK)[:, :, :, 2 * k : 2 * k + 2])
         scores = []
         for t in range(PACK):
             x_codes = sb.tile([P, P], U32, name="x_codes%d" % t, align_bytes=64)
             x_scales = sb.tile([P, P], U8, name="x_scales%d" % t, align_bytes=64)
-            nc.vector.quantize_mx(out=x_codes[:].bitcast(E4M3), scales=x_scales[:], in_=x_by_d[:, t * P * PACK : (t + 1) * P * PACK])
-            a = acc.tile([P, N], F32, name="acc_bank")
-            nc.tensor.matmul_mx(out=a[:], lhsT=x_codes[:].bitcast(E4M3), lhsT_scale=x_scales[:],
-                                rhs=wd_codes[:].bitcast(E4M3), rhs_scale=wd_scales[:], start=True, stop=True)
-            scores.append(a)
+            nc.vector.quantize_mx(out=x_codes[:].bitcast(E4M3), scales=x_scales[:], in_=x_by_d[t // 2][:, t % 2, :])
+            cuts = [slice(N // 2, N), slice(0, N // 2)] if t == 0 else [slice(0, N)]
+            parts = []
+            for n, cols in enumerate(cuts):
+                a = (turn if n == 1 else acc).tile([P, cols.stop - cols.start], F32, name="turn_bank" if n == 1 else "acc_bank")
+                nc.tensor.matmul_mx(out=a[:], lhsT=x_codes[:].bitcast(E4M3), lhsT_scale=x_scales[:],
+                                    rhs=wd_codes[:, cols].bitcast(E4M3), rhs_scale=wd_scales[:, cols], start=True, stop=True)
+                parts.append((cols, a))
+            scores.append(parts)
 
-        ws_codes = sb.tile([P, D], U32, name="ws_codes", align_bytes=64)
-        ws_scales = sb.tile([P, D], U8, name="ws_scales", align_bytes=64)
-        nc.vector.quantize_mx(out=ws_codes[:].bitcast(E4M3), scales=ws_scales[:], in_=w_by_slot[:])
+        quantise_by_slot(1)
 
         terms = []
         for t in range(PACK):
@@ -127,21 +139,26 @@ def tile_attend_gsq_pl_x_ts_kernel(tc, xT, wT, y, wt, ts, offs, out_0, out_1, ou
             nc.scalar.activation(target[:].rearrange("q (u s) -> q s u", u=PACK),
                                  y_raw[t][:].rearrange("q (s u) -> q s u", u=PACK), COPY, scale=neg_wt[:, t : t + 1])
             fitted = sb.tile([P, N], F32, name="fitted%d" % t)
-            nc.vector.scalar_tensor_tensor(fitted[:], scores[t][:], wt_cols[:, t : t + 1], ts_rows[:], MULT, MULT)
-            terms.append((target, fitted))
+            for cols, a in scores[t]:
+                nc.vector.scalar_tensor_tensor(fitted[:, cols], a[:], wt_cols[:, t : t + 1], ts_rows[:, cols], MULT, MULT)
+            summed = sb.tile([P, N - PE_SUMS * P], F32, name="summed%d" % t)
+            nc.gpsimd.tensor_tensor(summed[:], fitted[:, PE_SUMS * P :], target[:, PE_SUMS * P :], ADD)
+            terms.append((target, fitted, summed))
 
         g_banks = []
         for t in range(PACK):
             bank = turn.tile([P, PACK, P], F32, name="turn_bank")
-            for n, term in enumerate(terms[t]):
-                for u in range(PACK):
-                    nc.tensor.matmul(bank[:, u, :], lhsT=term[:, u * P : (u + 1) * P], rhs=ident[:], is_transpose=True,
-                                     start=(n == 0 and u == 0), stop=(n == 1 and u == PACK - 1))
+            target, fitted, summed = terms[t]
+            blocks = [(u, target[:, u * P : (u + 1) * P]) for u in range(PE_SUMS)]
+            blocks.extend((u, fitted[:, u * P : (u + 1) * P]) for u in range(PE_SUMS))
+            blocks.extend((u, summed[:, (u - PE_SUMS) * P : (u - PE_SUMS + 1) * P]) for u in range(PE_SUMS, PACK))
+            for n, (u, block) in enumerate(blocks):
+                nc.tensor.matmul(bank[:, u, :], lhsT=block, rhs=ident[:], is_transpose=True,
+                                 start=(n == 0), stop=(n == len(blocks) - 1))
             g_banks.append(bank)
 
         out_rows = out_0[0].rearrange("(q t) d -> q t d", t=PACK)
-        result = [sb.tile([P, 2, D], F32, name="result%d" % k) for k in range(2)]
-        o_by_row = sb.tile([P, D * PACK], BF16, name="o_by_row", align_bytes=64)
+        result = [sb.tile([P, 2 * D], F32, name="result%d" % k) for k in range(2)]
         h_tiles = []
 
         def weigh(t):
@@ -154,11 +171,18 @@ def tile_attend_gsq_pl_x_ts_kernel(tc, xT, wT, y, wt, ts, offs, out_0, out_1, ou
             h_codes = sb.tile([P, P], U32, name="h_codes%d" % t, align_bytes=64)
             h_scales = sb.tile([P, P], U8, name="h_scales%d" % t, align_bytes=64)
             nc.vector.quantize_mx(out=h_codes[:].bitcast(E5M2), scales=h_scales[:], in_=h_tiles[t][:])
-            gx = acc.tile([P, D], F32, name="acc_bank")
-            nc.tensor.matmul_mx(out=gx[:], lhsT=h_codes[:].bitcast(E5M2), lhsT_scale=h_scales[:],
-                                rhs=ws_codes[:].bitcast(E4M3), rhs_scale=ws_scales[:], start=True, stop=True)
-            nc.scalar.copy(result[t // 2][:, t % 2, :], gx[:])
-            nc.sync.dma_start(out=out_rows[:, t, :], in_=result[t // 2][:, t % 2, :])
+            pieces = 2 if t >= PACK - 2 else 1
+            width = D // pieces
+            for c in range(pieces):
+                cols = slice(c * width, (c + 1) * width)
+                gx = (turn if c == 1 else acc).tile([P, width], F32, name="turn_bank" if c == 1 else "acc_bank")
+                nc.tensor.matmul_mx(out=gx[:], lhsT=h_codes[:].bitcast(E5M2), lhsT_scale=h_scales[:],
+                                    rhs=ws_codes[:, cols].bitcast(E4M3), rhs_scale=ws_scales[:, cols], start=True, stop=True)
+                copy = nc.vector.tensor_copy if (t, c) == (PACK - 2, 1) else nc.scalar.copy
+                copy(
+                    result[t // 2][:, (t % 2) * D + c * width : (t % 2) * D + (c + 1) * width].rearrange("q (h p j) -> q h p j", p=P // 2, j=PACK),
+                    gx[:].rearrange("q (h j p) -> q h p j", j=PACK, p=P // 2))
+            nc.sync.dma_start(out=out_rows[:, t, :], in_=result[t // 2][:, (t % 2) * D : (t % 2 + 1) * D])
 
         weigh(0)
         for t in range(1, PACK):
@@ -166,13 +190,19 @@ def tile_attend_gsq_pl_x_ts_kernel(tc, xT, wT, y, wt, ts, offs, out_0, out_1, ou
             multiply(t - 1)
         multiply(PACK - 1)
 
-        o_view = o_by_row[:].rearrange("q (d t) -> q d t", t=PACK)
+        half = D // 2
+        o_by_row = [sb.tile([P, half * PACK], BF16, name="o_by_row%d" % c, align_bytes=64) for c in range(2)]
         for k in range(2):
-            nc.vector.tensor_copy(o_view[:, :, 2 * k : 2 * k + 2], result[k][:].rearrange("q e d -> q d e"))
+            for c in range(2):
+                nc.vector.tensor_copy(o_by_row[c][:].rearrange("q (d t) -> q d t", t=PACK)[:, :, 2 * k : 2 * k + 2],
+                                      result[k][:].rearrange("q (e d) -> q d e", e=2)[:, c * half : (c + 1) * half, :])
         o_codes = sb.tile([P, D], U32, name="o_codes", align_bytes=64)
         o_scales = sb.tile([P, D], U8, name="o_scales", align_bytes=64)
-        nc.vector.quantize_mx(out=o_codes[:].bitcast(E4M3), scales=o_scales[:], in_=o_by_row[:])
-        nc.sync.dma_start(out=out_1[0].rearrange("p d l -> p (d l)").bitcast(I32), in_=o_codes[:].bitcast(I32))
+        words_out = out_1[0].rearrange("p d l -> p (d l)").bitcast(I32)
+        for c in range(2):
+            cols = slice(c * half, (c + 1) * half)
+            nc.vector.quantize_mx(out=o_codes[:, cols].bitcast(E4M3), scales=o_scales[:, cols], in_=o_by_row[c][:])
+            nc.sync.dma_start(out=words_out[:, cols], in_=o_codes[:, cols].bitcast(I32))
         for quad in range(4):
             queue = nc.scalar if quad % 2 == 0 else nc.sync
             queue.dma_start(out=out_2[0, 4 * quad : 4 * quad + 4, :].bitcast(I32),

from contextlib import ExitStack

import concourse.mybir as mybir
from concourse.masks import make_identity

N, T, D, R = 512, 2048, 512, 512
P = 128
PACK = 4

F32 = mybir.dt.float32
BF16 = mybir.dt.bfloat16
I32 = mybir.dt.int32
U32 = mybir.dt.uint32
U16 = mybir.dt.uint16
U8 = mybir.dt.uint8
E4M3 = mybir.dt.float8_e4m3fn_x4
E5M2 = mybir.dt.float8_e5m2_x4
MULT = mybir.AluOpType.mult
ADD = mybir.AluOpType.add
COPY = mybir.ActivationFunctionType.Copy

FLOPS = 2 * 2 * R * N * D
BYTES = 4 * (D * R + D * T + R * N + R + T + R * D) + 2 * P * (N // 16) + R * D + (R // 32) * D

PE_SUMS = 2
VECTOR_COLS = 16


def tile_attend_gsq_pl_x_ts_kernel(tc, xT, wT, y, wt, ts, offs, out_0, out_1, out_2):
    nc = tc.nc
    with ExitStack() as ctx:
        sb = ctx.enter_context(tc.tile_pool(name="sb", bufs=1))
        acc = ctx.enter_context(tc.psum_pool(name="acc", bufs=4))
        turn = ctx.enter_context(tc.psum_pool(name="turn", bufs=4))

        w_planes = wT.rearrange("(p j) c -> p j c", j=PACK)
        w_raw = [sb.tile([P, T], F32, name="w_raw%d" % j, tag="w_raw%d" % j, align_bytes=64) for j in range(PACK)]
        nc.sync.dma_start(out=w_raw[0][:], in_=w_planes[:, 0, :])
        offsets = sb.tile([P, N // 16], U16, name="offsets")
        nc.sync.dma_start(offsets[:], offs)

        wt_cols = sb.tile([P, PACK], F32, name="wt_cols")
        nc.scalar.dma_start(out=wt_cols[:], in_=wt[0].rearrange("(q t) o -> q (t o)", t=PACK))
        ts_row = sb.tile([P, T], F32, name="ts_row")
        nc.vector.memset(ts_row[:, : T // 2], 0.0)
        nc.gpsimd.memset(ts_row[:, T // 2 :], 0.0)
        nc.sync.dma_start(out=ts_row[0:1, :], in_=ts[0:1, :])

        for j in range(1, PACK):
            nc.sync.dma_start(out=w_raw[j][:], in_=w_planes[:, j, :])
        x_planes = xT[0].rearrange("(p j) r -> p j r", j=PACK)
        x_raw = [sb.tile([P, PACK, R // 2], F32, name="x_raw%d" % h) for h in range(2)]
        for h in range(2):
            nc.sync.dma_start(out=x_raw[h][:], in_=x_planes[:, :, h * (R // 2) : (h + 1) * (R // 2)])
        y_rows = y[0].rearrange("(q t) i -> q t i", t=PACK)
        y_raw = [sb.tile([P, N], F32, name="y_raw%d" % t) for t in range(PACK)]
        for t in range(PACK):
            nc.sync.dma_start(out=y_raw[t][:], in_=y_rows[:, t, :])

        ident = sb.tile([P, P], F32, name="ident")
        make_identity(nc, ident[:])
        neg_wt = sb.tile([P, PACK], F32, name="neg_wt")
        nc.scalar.activation(neg_wt[:], wt_cols[:], COPY, scale=-1.0)

        ts_picked = sb.tile([P, N], F32, name="ts_picked")
        nc.scalar.activation(ts_picked[:], ts_row[:].indirect(offsets[:]), COPY)
        bank = turn.tile([P, PACK, P], F32, name="turn_bank")
        for u in range(PACK):
            nc.tensor.transpose(bank[:, u, :], ts_picked[:, u:N:PACK], ident[:])
        ts_cols = sb.tile([P, 1, PACK], F32, name="ts_cols")
        nc.scalar.copy(ts_cols[:, 0, :], bank[:, :, 0])
        bank = turn.tile([P, PACK, P], F32, name="turn_bank")
        for u in range(PACK):
            nc.tensor.transpose(bank[:, u, :], ts_cols[:, 0, u : u + 1].to_broadcast([P, P]), ident[:])
        ts_rows = sb.tile([P, N], F32, name="ts_rows")
        nc.scalar.copy(ts_rows[:], bank[:].rearrange("p u s -> p (u s)"))

        picked = [sb.tile([P, 2 * N], BF16, name="picked%d" % k, align_bytes=64) for k in range(2)]
        w_by_d = sb.tile([P, N * PACK], BF16, name="w_by_d", align_bytes=64)
        by_slot = [sb.tile([P, 2 * P * PACK], BF16, name="w_by_slot%d" % k, align_bytes=64) for k in range(2)]
        ws_codes = sb.tile([P, D], U32, name="ws_codes", tag="w_raw2", align_bytes=64)
        ws_scales = sb.tile([P, D], U8, name="ws_scales", align_bytes=64)
        for j in range(PACK):
            k, e = divmod(j, 2)
            plane = picked[k][:, e * N : (e + 1) * N]
            if j < PACK - 1:
                nc.vector.tensor_copy(plane, w_raw[j][:].indirect(offsets[:]))
            else:
                cut = 16 * VECTOR_COLS
                nc.vector.tensor_copy(plane[:, :cut], w_raw[j][:].indirect(offsets[:, :VECTOR_COLS]))
                nc.scalar.activation(plane[:, cut:], w_raw[j][:].indirect(offsets[:, VECTOR_COLS:]), COPY)
            if e == 1:
                nc.vector.tensor_copy(
                    w_by_d[:].rearrange("p (u s j) -> p s j u", u=PACK, j=PACK)[:, :, 2 * k : 2 * k + 2, :],
                    picked[k][:].rearrange("p (e s u) -> p s e u", e=2, u=PACK),
                )
            bank = turn.tile([P, 2, P], F32, name="turn_bank")
            for v in range(2):
                nc.tensor.transpose(bank[:, v, :], plane.bitcast(F32)[:, v : N // 2 : 2], ident[:])
            copy = nc.vector.tensor_copy if j == PACK - 1 else nc.scalar.copy
            copy(by_slot[k][:].bitcast(F32).rearrange("s (c e p v) -> s e c p v", c=2, e=2, v=2)[:, e],
                           bank[:].rearrange("s v (c p) -> s c p v", c=2))

        def quantise_by_slot(k):
            for c in range(2):
                cols = slice(c * (D // 2) + k * P, c * (D // 2) + (k + 1) * P)
                nc.vector.quantize_mx(out=ws_codes[:, cols].bitcast(E4M3), scales=ws_scales[:, cols],
                                      in_=by_slot[k][:, c * P * PACK : (c + 1) * P * PACK])

        quantise_by_slot(0)
        wd_codes = sb.tile([P, N], U32, name="wd_codes", align_bytes=64)
        wd_scales = sb.tile([P, N], U8, name="wd_scales", align_bytes=64)
        nc.vector.quantize_mx(out=wd_codes[:].bitcast(E4M3), scales=wd_scales[:], in_=w_by_d[:])

        x_by_d = [sb.tile([P, 2, P * PACK], BF16, name="x_by_d%d" % k, align_bytes=64) for k in range(2)]
        for h in range(2):
            for k in range(2):
                nc.scalar.copy(x_by_d[k][:].rearrange("p e (q j) -> p q j e", j=PACK)[:, h * (P // 2) : (h + 1) * (P // 2), :, :],
                     x_raw[h][:].rearrange("p j (q t) -> p q j t", t=PACK)[:, :, :, 2 * k : 2 * k + 2])
        scores = []
        for t in range(PACK):
            x_codes = sb.tile([P, P], U32, name="x_codes%d" % t, align_bytes=64)
            x_scales = sb.tile([P, P], U8, name="x_scales%d" % t, align_bytes=64)
            nc.vector.quantize_mx(out=x_codes[:].bitcast(E4M3), scales=x_scales[:], in_=x_by_d[t // 2][:, t % 2, :])
            cuts = [slice(N // 2, N), slice(0, N // 2)] if t == 0 else [slice(0, N)]
            parts = []
            for n, cols in enumerate(cuts):
                a = (turn if n == 1 else acc).tile([P, cols.stop - cols.start], F32, name="turn_bank" if n == 1 else "acc_bank")
                nc.tensor.matmul_mx(out=a[:], lhsT=x_codes[:].bitcast(E4M3), lhsT_scale=x_scales[:],
                                    rhs=wd_codes[:, cols].bitcast(E4M3), rhs_scale=wd_scales[:, cols], start=True, stop=True)
                parts.append((cols, a))
            scores.append(parts)

        quantise_by_slot(1)

        terms = []
        for t in range(PACK):
            target = sb.tile([P, N], F32, name="target%d" % t)
            nc.scalar.activation(target[:].rearrange("q (u s) -> q s u", u=PACK),
                                 y_raw[t][:].rearrange("q (s u) -> q s u", u=PACK), COPY, scale=neg_wt[:, t : t + 1])
            fitted = sb.tile([P, N], F32, name="fitted%d" % t)
            for cols, a in scores[t]:
                nc.vector.scalar_tensor_tensor(fitted[:, cols], a[:], wt_cols[:, t : t + 1], ts_rows[:, cols], MULT, MULT)
            summed = sb.tile([P, N - PE_SUMS * P], F32, name="summed%d" % t)
            nc.gpsimd.tensor_tensor(summed[:], fitted[:, PE_SUMS * P :], target[:, PE_SUMS * P :], ADD)
            terms.append((target, fitted, summed))

        g_banks = []
        for t in range(PACK):
            bank = turn.tile([P, PACK, P], F32, name="turn_bank")
            target, fitted, summed = terms[t]
            blocks = [(u, target[:, u * P : (u + 1) * P]) for u in range(PE_SUMS)]
            blocks.extend((u, fitted[:, u * P : (u + 1) * P]) for u in range(PE_SUMS))
            blocks.extend((u, summed[:, (u - PE_SUMS) * P : (u - PE_SUMS + 1) * P]) for u in range(PE_SUMS, PACK))
            for n, (u, block) in enumerate(blocks):
                nc.tensor.matmul(bank[:, u, :], lhsT=block, rhs=ident[:], is_transpose=True,
                                 start=(n == 0), stop=(n == len(blocks) - 1))
            g_banks.append(bank)

        out_rows = out_0[0].rearrange("(q t) d -> q t d", t=PACK)
        result = [sb.tile([P, 2 * D], F32, name="result%d" % k) for k in range(2)]
        h_tiles = []

        def weigh(t):
            h = sb.tile([P, P * PACK], BF16, name="h%d" % t, align_bytes=64)
            nc.vector.tensor_tensor(h[:].rearrange("s (q u) -> s q u", u=PACK), g_banks[t][:].rearrange("s u q -> s q u"),
                                    ts_cols[:].to_broadcast([P, P, PACK]), MULT)
            h_tiles.append(h)

        def multiply(t):
            h_codes = sb.tile([P, P], U32, name="h_codes%d" % t, align_bytes=64)
            h_scales = sb.tile([P, P], U8, name="h_scales%d" % t, align_bytes=64)
            nc.vector.quantize_mx(out=h_codes[:].bitcast(E5M2), scales=h_scales[:], in_=h_tiles[t][:])
            pieces = 2 if t >= PACK - 2 else 1
            width = D // pieces
            for c in range(pieces):
                cols = slice(c * width, (c + 1) * width)
                gx = (turn if c == 1 else acc).tile([P, width], F32, name="turn_bank" if c == 1 else "acc_bank")
                nc.tensor.matmul_mx(out=gx[:], lhsT=h_codes[:].bitcast(E5M2), lhsT_scale=h_scales[:],
                                    rhs=ws_codes[:, cols].bitcast(E4M3), rhs_scale=ws_scales[:, cols], start=True, stop=True)
                copy = nc.vector.tensor_copy if (t, c) == (PACK - 2, 1) else nc.scalar.copy
                copy(
                    result[t // 2][:, (t % 2) * D + c * width : (t % 2) * D + (c + 1) * width].rearrange("q (h p j) -> q h p j", p=P // 2, j=PACK),
                    gx[:].rearrange("q (h j p) -> q h p j", j=PACK, p=P // 2))
            nc.sync.dma_start(out=out_rows[:, t, :], in_=result[t // 2][:, (t % 2) * D : (t % 2 + 1) * D])

        weigh(0)
        for t in range(1, PACK):
            weigh(t)
            multiply(t - 1)
        multiply(PACK - 1)

        half = D // 2
        o_by_row = [sb.tile([P, half * PACK], BF16, name="o_by_row%d" % c, align_bytes=64) for c in range(2)]
        for k in range(2):
            for c in range(2):
                nc.vector.tensor_copy(o_by_row[c][:].rearrange("q (d t) -> q d t", t=PACK)[:, :, 2 * k : 2 * k + 2],
                                      result[k][:].rearrange("q (e d) -> q d e", e=2)[:, c * half : (c + 1) * half, :])
        o_codes = sb.tile([P, D], U32, name="o_codes", align_bytes=64)
        o_scales = sb.tile([P, D], U8, name="o_scales", align_bytes=64)
        words_out = out_1[0].rearrange("p d l -> p (d l)").bitcast(I32)
        for c in range(2):
            cols = slice(c * half, (c + 1) * half)
            nc.vector.quantize_mx(out=o_codes[:, cols].bitcast(E4M3), scales=o_scales[:, cols], in_=o_by_row[c][:])
            nc.sync.dma_start(out=words_out[:, cols], in_=o_codes[:, cols].bitcast(I32))
        for quad in range(4):
            queue = nc.scalar if quad % 2 == 0 else nc.sync
            queue.dma_start(out=out_2[0, 4 * quad : 4 * quad + 4, :].bitcast(I32),
                            in_=o_scales[32 * quad : 32 * quad + 4, :].bitcast(I32))
